import numpy as np
import ml_dtypes


def mxq(x, axis, fmt="e4m3"):
    dtype, down = {"e4m3": (ml_dtypes.float8_e4m3fn, 7), "e5m2": (ml_dtypes.float8_e5m2, 14)}[fmt]
    v = np.moveaxis(np.asarray(x, np.float32).astype(ml_dtypes.bfloat16).astype(np.float64), axis, -1)
    blocks = v.reshape(v.shape[:-1] + (-1, 32))
    amax = np.abs(blocks).max(-1, keepdims=True)
    byte = np.maximum(np.where(amax > 0, np.frexp(amax)[1] - 1 + 127, 0) - down, 1)
    scale = np.exp2(byte - 127.0)
    codes = (blocks / scale).astype(np.float32).astype(dtype).astype(np.float64)
    return np.moveaxis((codes * scale).reshape(v.shape), -1, axis)


WIDE = False


def mx_kscale(k):
    if not WIDE:
        return np.ones(k)
    levels = np.array([10, -10, 5, -5, 0])
    if k % 512:
        return np.exp2(np.random.permutation(np.resize(levels, k // 32))).repeat(32)
    a = np.empty((k // 512, 16))
    for p in range(k // 512):
        a[p, :8] = np.random.permutation(np.resize(levels, 8))
        for g in range(8):
            far = levels[np.abs(levels - a[p, g]) >= 10]
            a[p, g + 8] = far[np.random.randint(len(far))]
    return np.exp2(a.ravel()).repeat(32)


def f64(x):
    return np.asarray(x).astype(np.float64)


def striped(idx):
    return np.tile(idx.reshape(-1, 16).T, (8, 1)).astype(np.uint16)


def unstriped(offs):
    return offs[:16].T.reshape(-1).astype(np.int64)


def striped8(idx):
    return np.concatenate([x.reshape(-1, 16).T for x in idx]).astype(np.uint16)


def runs(offs, k):
    lists = np.stack([offs[16 * r : 16 * r + 16].T.reshape(-1) for r in range(8)]).astype(np.int64)
    return lists[np.arange(k) % 512 // 64]


def pack_weight(w):
    k, n = w.shape
    w = f64(np.asarray(w, np.float32).astype(ml_dtypes.bfloat16)).reshape(k // 32, 32, n)
    amax = np.abs(w).max(1)
    byte = np.clip(np.where(amax > 0, np.frexp(amax)[1] - 1 + 127 - 7, 1), 1, 254)
    scaled = (w * np.exp2(127.0 - byte)[:, None, :]).reshape(k, n).astype(np.float32)
    words = np.ascontiguousarray(scaled.reshape(k // 512, 128, 4, n).transpose(0, 1, 3, 2)).astype(ml_dtypes.float8_e4m3fn).view(np.uint8)
    return words, np.ascontiguousarray(byte.astype(np.uint8).reshape(k // 512, 16, n))


def unpack_weight(words, scales):
    g, p, n, _ = words.shape
    vals = np.ascontiguousarray(words).view(ml_dtypes.float8_e4m3fn).astype(np.float64) * np.repeat(np.exp2(scales.astype(np.float64) - 127.0), 8, axis=1)[..., None]
    return vals.transpose(0, 1, 3, 2).reshape(g * 512, n)


def relu(v):
    return np.maximum(v, 0.0)


def sigmoid(v):
    return 1.0 / (1.0 + np.exp(-np.maximum(v, -700.0)))

def planes(y):
    n, m = y.shape
    v = y.astype(np.float32).astype(ml_dtypes.bfloat16).astype(np.float64).reshape(n // 32, 32, m)
    top = np.abs(v).max(1)
    byte = np.clip(np.where(top > 0, np.frexp(top)[1] - 1 + 127 - 7, 1), 1, 254)
    codes = (v * np.exp2(127.0 - byte)[:, None, :]).reshape(n, m).astype(np.float32).astype(ml_dtypes.float8_e4m3fn).view(np.uint8)
    words = codes.reshape(n // 512, 128, 4, m).transpose(0, 1, 3, 2)
    return np.ascontiguousarray(words), np.ascontiguousarray(byte.astype(np.uint8).reshape(n // 512, 16, m))


K, T, S, N, H = 512, 2048, 512, 512, 512


def setup_inputs():
    n = np.random.standard_normal
    s = mx_kscale(K)[:, None]
    u = mx_kscale(H)
    packed_xT = pack_weight(n((K, T)) * s)
    packed_w1 = pack_weight(n((K, H)) / np.sqrt(K) / s)
    packed_w2 = pack_weight(n((H, N)) / np.sqrt(2 * H) / u[:, None])
    packed_w3 = pack_weight(n((H, N)) / np.sqrt(2 * H) / u[:, None])
    return {
        "x_words": packed_xT[0],
        "x_scales": packed_xT[1],
        "w1_words": packed_w1[0],
        "w1_scales": packed_w1[1],
        "gn": (np.random.uniform(0.5, 1.5, (H, 1)) * u[:, None]).astype(np.float32),
        "gm": (np.random.uniform(0.5, 1.5, (H, 1)) * u[:, None]).astype(np.float32),
        "w2_words": packed_w2[0],
        "w2_scales": packed_w2[1],
        "w3_words": packed_w3[0],
        "w3_scales": packed_w3[1],
        "offs": striped(np.random.permutation(T)[:S]),
        "n1": striped8(np.stack([np.random.permutation(S) for _ in range(8)])),
        "n2": striped8(np.stack([np.random.permutation(S) for _ in range(8)])),
        "n3": striped8(np.stack([np.random.permutation(S) for _ in range(8)])),
        "n4": striped8(np.stack([np.random.permutation(S) for _ in range(8)])),
        "n5": striped8(np.stack([np.random.permutation(S) for _ in range(8)])),
        "n6": striped8(np.stack([np.random.permutation(S) for _ in range(8)])),
    }


def reference(x_words, x_scales, w1_words, w1_scales, gn, gm, w2_words, w2_scales, w3_words, w3_scales, offs, n1, n2, n3, n4, n5, n6):
    xq = unpack_weight(x_words, x_scales)[:, unstriped(offs)]
    y = unpack_weight(w1_words, w1_scales).T @ xq
    rl = relu(y)
    ds = np.zeros((H, S))
    ds[np.arange(H)[:, None], runs(n1, H)] = rl
    z = f64(gn) * (ds - (0.5 * y))
    pa = y[np.arange(H)[:, None], runs(n2, H)]
    z2 = f64(gm) * (pa + (sigmoid(y[np.arange(H)[:, None], runs(n3, H)])) * (y[np.arange(H)[:, None], runs(n4, H)] - pa))
    h = unpack_weight(w2_words, w2_scales).T @ mxq(z, 0, "e4m3") + unpack_weight(w3_words, w3_scales).T @ mxq(z2, 0, "e4m3")
    out_0 = 0.75 * ((h - (h[np.arange(N)[:, None], runs(n5, N)])) * (h - (h[np.arange(N)[:, None], runs(n6, N)])))
    return (out_0,) + planes(out_0)

@@ -1,0 +1,303 @@
+from contextlib import ExitStack
+
+import concourse.mybir as mybir
+from concourse.masks import make_identity
+
+K, T, S, H, N = 512, 2048, 512, 512, 512
+FLOPS = 2 * K * H * S + 2 * 2 * H * N * S
+
+F32 = mybir.dt.float32
+BF16 = mybir.dt.bfloat16
+I32 = mybir.dt.int32
+U32 = mybir.dt.uint32
+U16 = mybir.dt.uint16
+U8 = mybir.dt.uint8
+FP8X4 = mybir.dt.float8_e4m3fn_x4
+ALU = mybir.AluOpType
+ACT = mybir.ActivationFunctionType
+
+P = 128
+PACK = 4
+STRIPE = 16
+CHUNKS = ((0, 256), (256, 384), (384, 512))
+
+
+def entries(tile, lo, hi):
+    return tile[:, lo // STRIPE : hi // STRIPE]
+
+
+def load_words(nc, tile, words):
+    nc.sync.dma_start(out=tile[:], in_=words[0].rearrange("p n t -> p (n t)").bitcast(I32))
+
+
+def load_scales(queues, tile, scales, first):
+    for q, queue in enumerate(queues):
+        queue.dma_start(
+            out=tile[32 * q + first : 32 * q + first + 4, :].bitcast(I32),
+            in_=scales[0, 4 * q : 4 * q + 4, :].bitcast(I32),
+        )
+
+
+def deal_columns(nc, dst, src, run):
+    nc.vector.tensor_copy(
+        out=dst[:].rearrange("p (t c i) -> p c t i", t=PACK, i=run),
+        in_=src[:].rearrange("p (c i t) -> p c t i", t=PACK, i=run),
+    )
+
+
+def tile_picked_joinsendlerpquad_none_po_kernel(
+    tc, x_words, x_scales, w1_words, w1_scales, gn, gm, w2_words, w2_scales, w3_words, w3_scales,
+    offs, n1, n2, n3, n4, n5, n6, out_0, out_1, out_2,
+):
+    nc = tc.nc
+    with ExitStack() as ctx:
+        keep = ctx.enter_context(tc.tile_pool(name="keep", bufs=1))
+        sums = ctx.enter_context(tc.psum_pool(name="sums", bufs=1))
+        turns = ctx.enter_context(tc.psum_pool(name="turns", bufs=4))
+
+        def sb(name, width, dtype, tag=None):
+            return keep.tile([P, width], dtype, name=name, tag=tag or name, align_bytes=64)
+
+        xw = sb("xw", T, I32)
+        xs = sb("xs", T, U8)
+        w1w = sb("w1w", H, I32)
+        w1s = sb("w1s", H, U8)
+        w2w = sb("w2w", N, I32)
+        w3w = sb("w3w", N, I32)
+        w23s = sb("w23s", N, U8)
+        gains = sb("gains", PACK, F32)
+        gains_m = sb("gains_m", PACK, F32)
+        lists = [keep.tile([P, S // STRIPE], U16, name="list%d" % a) for a in range(7)]
+        l0, l1, l2, l3, l4, l5, l6 = lists
+
+        nc.gpsimd.memset(w1s[:].bitcast(I32), 0)
+        nc.vector.memset(xs[:].bitcast(I32), 0)
+        nc.vector.memset(w23s[:].bitcast(I32), 0)
+        warm = sb("warm", 2, F32)
+        nc.vector.memset(warm[:, 0:1], 0.0)
+        nc.scalar.activation(out=warm[:, 1:2], in_=warm[:, 0:1], func=ACT.Sigmoid)
+
+        on_sync = [nc.sync] * 4
+        nc.sync.dma_start(l0[:], offs)
+        nc.sync.dma_start(l1[:], n1)
+        load_words(nc, w1w, w1_words)
+        load_words(nc, xw, x_words)
+        load_scales(on_sync, xs, x_scales, 0)
+        nc.gpsimd.dma_start(out=gains[:, 0:PACK], in_=gn.rearrange("(p t) o -> p (t o)", t=PACK))
+        load_scales([nc.sync, nc.sync, nc.sync, nc.gpsimd], w1s, w1_scales, 0)
+        nc.sync.dma_start(out=gains_m[:], in_=gm.rearrange("(p t) o -> p (t o)", t=PACK))
+        nc.sync.dma_start(l3[:], n3)
+        load_words(nc, w2w, w2_words)
+        load_words(nc, w3w, w3_words)
+        load_scales(on_sync, w23s, w2_scales, 0)
+        load_scales(on_sync, w23s, w3_scales, 4)
+        nc.sync.dma_start(l4[:], n4)
+        nc.sync.dma_start(l2[:], n2)
+        nc.sync.dma_start(l5[:], n5)
+        nc.sync.dma_start(l6[:], n6)
+
+        ident = sb("ident", P, F32)
+        make_identity(nc, ident[:])
+
+        gn_wide = sb("gn_wide", PACK * S, F32)
+        nc.scalar.copy(
+            out=gn_wide[:].rearrange("p (t j) -> p t j", t=PACK),
+            in_=gains[:, 0:PACK].unsqueeze(2).to_broadcast([P, PACK, S]),
+        )
+        gn_half = sb("gn_half", PACK, F32)
+        nc.scalar.activation(out=gn_half[:], in_=gains[:, 0:PACK], func=ACT.Copy, scale=-0.5)
+
+        w1d = sb("w1d", H, I32)
+        w1ds = sb("w1ds", H, U8)
+        deal_columns(nc, w1d, w1w, 4)
+        xg = sb("xg", S, U32)
+        xgs = sb("xgs", S, U8)
+        nc.vector.tensor_copy(out=xgs[:], in_=xs[:].indirect(l0[:]))
+        deal_columns(nc, w1ds, w1s, 16)
+        halves = ((0, S // 2), (S // 2, S))
+        for lo, hi in halves:
+            nc.vector.tensor_copy(out=xg[:, lo:hi], in_=xw[:].bitcast(U32).indirect(entries(l0, lo, hi)))
+
+        y_ps = [sums.tile([P, S], F32, name="y_ps%d" % t, tag="sum%d" % t) for t in range(PACK)]
+        rl = [sb("rl%d" % t, S, F32) for t in range(PACK)]
+        ds = [sb("ds%d" % t, 2 * S, F32) for t in range(PACK)]
+        for t in range(PACK):
+            cols = slice(P * t, P * (t + 1))
+            for lo, hi in halves if t == 0 else ((0, S),):
+                nc.tensor.matmul_mx(
+                    out=y_ps[t][:, lo:hi], lhsT=w1d[:, cols].bitcast(FP8X4), lhsT_scale=w1ds[:, cols],
+                    rhs=xg[:, lo:hi].bitcast(FP8X4), rhs_scale=xgs[:, lo:hi], start=True, stop=True,
+                )
+                nc.scalar.activation(out=rl[t][:, lo:hi], in_=y_ps[t][:, lo:hi], func=ACT.Relu)
+                nc.vector.tensor_tensor(
+                    ds[t][:].indirect(entries(l1, lo, hi)), rl[t][:, lo:hi],
+                    gn_wide[:, S * t + lo : S * t + hi], ALU.mult,
+                )
+
+        w2d = sb("w2d", N, I32)
+        w3d = sb("w3d", N, I32)
+        w23ds = sb("w23ds", N, U8)
+        deal_columns(nc, w2d, w2w, 4)
+        deal_columns(nc, w3d, w3w, 4)
+        deal_columns(nc, w23ds, w23s, 16)
+
+        y = [sb("y%d" % t, S, F32) for t in range(PACK)]
+        yg = [sb("yg%d" % t, S, F32) for t in range(PACK)]
+        yh = [sb("yh%d" % t, S, F32) for t in range(PACK)]
+        gate = [sb("gate%d" % c, PACK * (hi - lo), F32) for c, (lo, hi) in enumerate(CHUNKS)]
+        rest = [sb("rest%d" % c, PACK * (hi - lo), F32) for c, (lo, hi) in enumerate(CHUNKS)]
+
+        def gate_of(c, t):
+            lo, hi = CHUNKS[c]
+            w = hi - lo
+            nc.scalar.activation(
+                out=gate[c][:, w * t : w * (t + 1)], in_=y[t][:].indirect(entries(l3, lo, hi)), func=ACT.Sigmoid,
+            )
+
+        def rest_of(c):
+            nc.scalar.activation(out=rest[c][:], in_=gate[c][:], func=ACT.Copy, scale=-1.0, bias=1.0)
+
+        for t in range(PACK):
+            nc.scalar.copy(out=y[t][:], in_=y_ps[t][:])
+            nc.scalar.activation(out=yg[t][:], in_=y_ps[t][:], func=ACT.Copy, scale=gains_m[:, t : t + 1])
+            gate_of(0, t)
+        rest_of(0)
+        for t in range(PACK):
+            nc.scalar.activation(out=yh[t][:], in_=y_ps[t][:], func=ACT.Copy, scale=gn_half[:, t : t + 1])
+        for c in (1, 2):
+            for t in range(PACK):
+                gate_of(c, t)
+            rest_of(c)
+
+        def terms(c, tag_a, tag_b):
+            lo, hi = CHUNKS[c]
+            w = hi - lo
+            far = sb("far%d" % c, PACK * w, F32, tag_b)
+            near = sb("near%d" % c, PACK * w, F32, tag_a)
+            for t in range(PACK):
+                cols = slice(w * t, w * (t + 1))
+                nc.vector.tensor_tensor(far[:, cols], yg[t][:].indirect(entries(l4, lo, hi)), gate[c][:, cols], ALU.mult)
+            for t in range(PACK):
+                cols = slice(w * t, w * (t + 1))
+                nc.vector.tensor_tensor(near[:, cols], yg[t][:].indirect(entries(l2, lo, hi)), rest[c][:, cols], ALU.mult)
+            return far, near
+
+        def add_turned(pairs, blocks, name):
+            banks = [turns.tile([P, PACK * P], F32, name="%s_sum%d" % (name, b), tag="turn") for b in blocks]
+            for t in range(PACK):
+                for bank, b in zip(banks, blocks):
+                    for a in range(2):
+                        nc.tensor.matmul(
+                            bank[:, P * t : P * (t + 1)], pairs[t][a][:, P * b : P * (b + 1)], ident[:],
+                            start=(a == 0), stop=(a == 1), is_transpose=True,
+                        )
+            return banks
+
+        def round_and_turn_back(banks, name, tag):
+            turned = []
+            for b, bank in enumerate(banks):
+                pairs16 = sb("%s_pairs%d" % (name, b), PACK * P, BF16)
+                nc.scalar.copy(
+                    out=pairs16[:].rearrange("j (u p e) -> j u p e", u=2, e=2),
+                    in_=bank[:].rearrange("j (u e p) -> j u p e", u=2, e=2),
+                )
+                turned.append(pairs16)
+            w = P * len(banks)
+            back = turns.tile([P, 2 * w], F32, name="%s_back" % name, tag="turn")
+            for b, pairs16 in enumerate(turned):
+                for u in range(2):
+                    nc.tensor.transpose(
+                        back[:, w * u + P * b : w * u + P * (b + 1)],
+                        pairs16[:].bitcast(F32)[:, P * u : P * (u + 1)], ident[:],
+                    )
+            grouped = sb("%s_grouped" % name, PACK * w, BF16, tag)
+            nc.scalar.copy(
+                out=grouped[:].bitcast(F32).rearrange("p (j u) -> p j u", u=2),
+                in_=back[:].rearrange("p (u j) -> p j u", u=2),
+            )
+            return grouped
+
+        def quantise(words, scales, lo, hi, grouped):
+            nc.vector.quantize_mx(out=words[:, lo:hi].bitcast(FP8X4), scales=scales[:, lo:hi], in_=grouped[:])
+
+        zq = sb("zq", S, U32)
+        zqs = sb("zqs", S, U8)
+        z2q = sb("z2q", S, U32)
+        z2qs = sb("z2qs", S, U8)
+
+        z_banks = add_turned([[yh[t][:], ds[t][:, 0:S]] for t in range(PACK)], range(4), "z")
+        terms0 = terms(0, None, None)
+        terms1 = terms(1, None, None)
+        for a, (lo, hi) in enumerate(halves):
+            quantise(zq, zqs, lo, hi, round_and_turn_back(z_banks[2 * a : 2 * a + 2], "z%d" % a, "ring%d" % a))
+        terms2 = terms(2, "ring1", "ring0")
+
+        h_ps = [sums.tile([P, S], F32, name="h_ps%d" % t, tag="sum%d" % t) for t in range(PACK)]
+        h = [sb("h%d" % t, S, F32) for t in range(PACK)]
+        h_own = [sb("h_own%d" % t, S, F32) for t in range(PACK)]
+
+        def second_product(c):
+            lo, hi = CHUNKS[c]
+            for t in range(PACK):
+                cols = slice(P * t, P * (t + 1))
+                nc.tensor.matmul_mx(
+                    out=h_ps[t][:, lo:hi], lhsT=w2d[:, cols].bitcast(FP8X4), lhsT_scale=w23ds[:, cols],
+                    rhs=zq[:, lo:hi].bitcast(FP8X4), rhs_scale=zqs[:, lo:hi], start=True, stop=False,
+                )
+                nc.tensor.matmul_mx(
+                    out=h_ps[t][:, lo:hi], lhsT=w3d[:, cols].bitcast(FP8X4), lhsT_scale=w23ds[4:P, cols],
+                    rhs=z2q[:, lo:hi].bitcast(FP8X4), rhs_scale=z2qs[:, lo:hi], start=False, stop=True,
+                )
+
+        def h_out(t, lo, hi):
+            nc.scalar.copy(out=h[t][:, lo:hi], in_=h_ps[t][:, lo:hi])
+            nc.scalar.copy(out=h_own[t][:, lo:hi], in_=h_ps[t][:, lo:hi])
+
+        for c, both in ((0, terms0), (1, terms1)):
+            lo, hi = CHUNKS[c]
+            pairs = [[term[:, (hi - lo) * t : (hi - lo) * (t + 1)] for term in both] for t in range(PACK)]
+            banks = add_turned(pairs, range((hi - lo) // P), "z2_%d" % c)
+            quantise(z2q, z2qs, lo, hi, round_and_turn_back(banks, "z2_%d" % c, "ring2" if c == 0 else None))
+            second_product(c)
+        h_out(0, 0, CHUNKS[1][1])
+
+        lo, hi = CHUNKS[2]
+        grouped = sb("z2_2_grouped", PACK * (hi - lo), BF16, "ring2")
+        nc.vector.tensor_tensor(
+            grouped[:].rearrange("p (c i t) -> p c t i", t=PACK, i=4),
+            terms2[0][:].rearrange("p (t c i) -> p c t i", t=PACK, i=4),
+            terms2[1][:].rearrange("p (t c i) -> p c t i", t=PACK, i=4),
+            ALU.add,
+        )
+        quantise(z2q, z2qs, lo, hi, grouped)
+        second_product(2)
+        h_out(0, lo, hi)
+        for t in range(1, PACK):
+            h_out(t, 0, S)
+
+        oq = sb("oq", S, U32)
+        oqs = sb("oqs", S, U8)
+        out_rows = out_0.rearrange("(p t) j -> p t j", t=PACK)
+        out_words = out_1[0].rearrange("p n t -> p (n t)").bitcast(I32)
+        for c, (lo, hi) in enumerate(CHUNKS):
+            w = hi - lo
+            d5 = sb("d5_%d" % c, PACK * w, F32)
+            d6 = sb("d6_%d" % c, PACK * w, F32)
+            res = sb("res%d" % c, PACK * w, F32)
+            for t in range(PACK):
+                cols = slice(w * t, w * (t + 1))
+                nc.vector.tensor_tensor(d5[:, cols], h[t][:].indirect(entries(l5, lo, hi)), h_own[t][:, lo:hi], ALU.subtract)
+                nc.vector.tensor_tensor(d6[:, cols], h[t][:].indirect(entries(l6, lo, hi)), h_own[t][:, lo:hi], ALU.subtract)
+            nc.vector.scalar_tensor_tensor(out=res[:], in0=d5[:], scalar=0.75, in1=d6[:], op0=ALU.mult, op1=ALU.mult)
+            nc.sync.dma_start(out=out_rows[:, :, lo:hi], in_=res[:].rearrange("p (t j) -> p t j", t=PACK))
+            res16 = sb("res16_%d" % c, PACK * w, BF16)
+            copy = nc.vector.tensor_copy if c == len(CHUNKS) - 1 else nc.scalar.copy
+            copy(
+                out=res16[:].rearrange("p (c i t) -> p c t i", t=PACK, i=4),
+                in_=res[:].rearrange("p (t c i) -> p c t i", t=PACK, i=4),
+            )
+            quantise(oq, oqs, lo, hi, res16)
+            nc.sync.dma_start(out=out_words[:, lo:hi], in_=oq[:, lo:hi].bitcast(I32))
+        for q in range(4):
+            queue = nc.sync if q % 2 == 0 else nc.scalar
+            queue.dma_start(out=out_2[0, 4 * q : 4 * q + 4, :].bitcast(I32), in_=oqs[32 * q : 32 * q + 4, :].bitcast(I32))

@@ -38,10 +38,10 @@ def load_scales(queues, tile, scales, first):
         )
 
 
-def deal_columns(nc, dst, src, run):
+def deal_columns(nc, dst, src, run, first=0, last=PACK):
     nc.vector.tensor_copy(
-        out=dst[:].rearrange("p (t c i) -> p c t i", t=PACK, i=run),
-        in_=src[:].rearrange("p (c i t) -> p c t i", t=PACK, i=run),
+        out=dst[:].rearrange("p (t c i) -> p c t i", t=last - first, i=run),
+        in_=src[:].rearrange("p (c i t) -> p c t i", t=PACK, i=run)[:, :, first:last, :],
     )
 
 
@@ -70,21 +70,21 @@ def tile_picked_joinsendlerpquad_none_po_kernel(
         lists = [keep.tile([P, S // STRIPE], U16, name="list%d" % a) for a in range(7)]
         l0, l1, l2, l3, l4, l5, l6 = lists
 
+        nc.gpsimd.memset(xs[:].bitcast(I32), 0)
         nc.gpsimd.memset(w1s[:].bitcast(I32), 0)
-        nc.vector.memset(xs[:].bitcast(I32), 0)
+        nc.gpsimd.dma_start(out=gains[:], in_=gn.rearrange("(p t) o -> p (t o)", t=PACK))
         nc.vector.memset(w23s[:].bitcast(I32), 0)
         warm = sb("warm", 2, F32)
         nc.vector.memset(warm[:, 0:1], 0.0)
         nc.scalar.activation(out=warm[:, 1:2], in_=warm[:, 0:1], func=ACT.Sigmoid)
 
         on_sync = [nc.sync] * 4
+        load_scales(on_sync, xs, x_scales, 0)
         nc.sync.dma_start(l0[:], offs)
-        nc.sync.dma_start(l1[:], n1)
         load_words(nc, w1w, w1_words)
         load_words(nc, xw, x_words)
-        load_scales(on_sync, xs, x_scales, 0)
-        nc.gpsimd.dma_start(out=gains[:, 0:PACK], in_=gn.rearrange("(p t) o -> p (t o)", t=PACK))
-        load_scales([nc.sync, nc.sync, nc.sync, nc.gpsimd], w1s, w1_scales, 0)
+        load_scales(on_sync, w1s, w1_scales, 0)
+        nc.sync.dma_start(l1[:], n1)
         nc.sync.dma_start(out=gains_m[:], in_=gm.rearrange("(p t) o -> p (t o)", t=PACK))
         nc.sync.dma_start(l3[:], n3)
         load_words(nc, w2w, w2_words)
@@ -99,11 +99,9 @@ def tile_picked_joinsendlerpquad_none_po_kernel(
         ident = sb("ident", P, F32)
         make_identity(nc, ident[:])
 
-        gn_wide = sb("gn_wide", PACK * S, F32)
-        nc.scalar.copy(
-            out=gn_wide[:].rearrange("p (t j) -> p t j", t=PACK),
-            in_=gains[:, 0:PACK].unsqueeze(2).to_broadcast([P, PACK, S]),
-        )
+        gn_wide = [sb("gn_wide%d" % t, S, F32) for t in range(PACK)]
+        for t in range(PACK):
+            nc.scalar.copy(out=gn_wide[t][:], in_=gains[:, t : t + 1].to_broadcast([P, S]))
         gn_half = sb("gn_half", PACK, F32)
         nc.scalar.activation(out=gn_half[:], in_=gains[:, 0:PACK], func=ACT.Copy, scale=-0.5)
 
@@ -131,15 +129,20 @@ def tile_picked_joinsendlerpquad_none_po_kernel(
                 nc.scalar.activation(out=rl[t][:, lo:hi], in_=y_ps[t][:, lo:hi], func=ACT.Relu)
                 nc.vector.tensor_tensor(
                     ds[t][:].indirect(entries(l1, lo, hi)), rl[t][:, lo:hi],
-                    gn_wide[:, S * t + lo : S * t + hi], ALU.mult,
+                    gn_wide[t][:, lo:hi], ALU.mult,
                 )
 
-        w2d = sb("w2d", N, I32)
-        w3d = sb("w3d", N, I32)
-        w23ds = sb("w23ds", N, U8)
-        deal_columns(nc, w2d, w2w, 4)
-        deal_columns(nc, w3d, w3w, 4)
-        deal_columns(nc, w23ds, w23s, 16)
+        def deal_second_weights(first, last, tags):
+            w = P * (last - first)
+            w2d = sb("w2d%d" % first, w, I32, tags[0])
+            w3d = sb("w3d%d" % first, w, I32, tags[1])
+            w23ds = sb("w23ds%d" % first, w, U8, tags[2])
+            deal_columns(nc, w2d, w2w, 4, first, last)
+            deal_columns(nc, w3d, w3w, 4, first, last)
+            deal_columns(nc, w23ds, w23s, 16, first, last)
+            return w2d, w3d, w23ds
+
+        dealt_first = deal_second_weights(0, 1, (None, None, None))
 
         y = [sb("y%d" % t, S, F32) for t in range(PACK)]
         yg = [sb("yg%d" % t, S, F32) for t in range(PACK)]
@@ -164,10 +167,9 @@ def tile_picked_joinsendlerpquad_none_po_kernel(
         rest_of(0)
         for t in range(PACK):
             nc.scalar.activation(out=yh[t][:], in_=y_ps[t][:], func=ACT.Copy, scale=gn_half[:, t : t + 1])
-        for c in (1, 2):
-            for t in range(PACK):
-                gate_of(c, t)
-            rest_of(c)
+        for t in range(PACK):
+            gate_of(1, t)
+        rest_of(1)
 
         def terms(c, tag_a, tag_b):
             lo, hi = CHUNKS[c]
@@ -230,50 +232,49 @@ def tile_picked_joinsendlerpquad_none_po_kernel(
         terms1 = terms(1, None, None)
         for a, (lo, hi) in enumerate(halves):
             quantise(zq, zqs, lo, hi, round_and_turn_back(z_banks[2 * a : 2 * a + 2], "z%d" % a, "ring%d" % a))
+        for t in range(PACK):
+            gate_of(2, t)
+        rest_of(2)
         terms2 = terms(2, "ring1", "ring0")
 
         h_ps = [sums.tile([P, S], F32, name="h_ps%d" % t, tag="sum%d" % t) for t in range(PACK)]
         h = [sb("h%d" % t, S, F32) for t in range(PACK)]
         h_own = [sb("h_own%d" % t, S, F32) for t in range(PACK)]
 
-        def second_product(c):
+        def second_product(t, lo, hi, dealt, at, acc):
+            w2d, w3d, w23ds = dealt
+            cols = slice(P * at, P * (at + 1))
+            nc.tensor.matmul_mx(
+                out=acc, lhsT=w2d[:, cols].bitcast(FP8X4), lhsT_scale=w23ds[:, cols],
+                rhs=zq[:, lo:hi].bitcast(FP8X4), rhs_scale=zqs[:, lo:hi], start=True, stop=False,
+            )
+            nc.tensor.matmul_mx(
+                out=acc, lhsT=w3d[:, cols].bitcast(FP8X4), lhsT_scale=w23ds[4:P, cols],
+                rhs=z2q[:, lo:hi].bitcast(FP8X4), rhs_scale=z2qs[:, lo:hi], start=False, stop=True,
+            )
+            nc.scalar.copy(out=h[t][:, lo:hi], in_=acc)
+            nc.scalar.copy(out=h_own[t][:, lo:hi], in_=acc)
+
+        lo, hi = CHUNKS[0]
+        pairs = [[term[:, (hi - lo) * t : (hi - lo) * (t + 1)] for term in terms0] for t in range(PACK)]
+        banks = add_turned(pairs, range((hi - lo) // P), "z2")
+        quantise(z2q, z2qs, lo, hi, round_and_turn_back(banks, "z2", "ring2"))
+        second_product(0, lo, hi, dealt_first, 0, h_ps[0][:, lo:hi])
+        for c, both in ((1, terms1), (2, terms2)):
             lo, hi = CHUNKS[c]
-            for t in range(PACK):
-                cols = slice(P * t, P * (t + 1))
-                nc.tensor.matmul_mx(
-                    out=h_ps[t][:, lo:hi], lhsT=w2d[:, cols].bitcast(FP8X4), lhsT_scale=w23ds[:, cols],
-                    rhs=zq[:, lo:hi].bitcast(FP8X4), rhs_scale=zqs[:, lo:hi], start=True, stop=False,
-                )
-                nc.tensor.matmul_mx(
-                    out=h_ps[t][:, lo:hi], lhsT=w3d[:, cols].bitcast(FP8X4), lhsT_scale=w23ds[4:P, cols],
-                    rhs=z2q[:, lo:hi].bitcast(FP8X4), rhs_scale=z2qs[:, lo:hi], start=False, stop=True,
-                )
-
-        def h_out(t, lo, hi):
-            nc.scalar.copy(out=h[t][:, lo:hi], in_=h_ps[t][:, lo:hi])
-            nc.scalar.copy(out=h_own[t][:, lo:hi], in_=h_ps[t][:, lo:hi])
-
-        for c, both in ((0, terms0), (1, terms1)):
-            lo, hi = CHUNKS[c]
-            pairs = [[term[:, (hi - lo) * t : (hi - lo) * (t + 1)] for term in both] for t in range(PACK)]
-            banks = add_turned(pairs, range((hi - lo) // P), "z2_%d" % c)
-            quantise(z2q, z2qs, lo, hi, round_and_turn_back(banks, "z2_%d" % c, "ring2" if c == 0 else None))
-            second_product(c)
-        h_out(0, 0, CHUNKS[1][1])
-
-        lo, hi = CHUNKS[2]
-        grouped = sb("z2_2_grouped", PACK * (hi - lo), BF16, "ring2")
-        nc.vector.tensor_tensor(
-            grouped[:].rearrange("p (c i t) -> p c t i", t=PACK, i=4),
-            terms2[0][:].rearrange("p (t c i) -> p c t i", t=PACK, i=4),
-            terms2[1][:].rearrange("p (t c i) -> p c t i", t=PACK, i=4),
-            ALU.add,
-        )
-        quantise(z2q, z2qs, lo, hi, grouped)
-        second_product(2)
-        h_out(0, lo, hi)
+            grouped = sb("z2_grouped%d" % c, PACK * (hi - lo), BF16, "ring2" if c == 2 else None)
+            nc.vector.tensor_tensor(
+                grouped[:].rearrange("p (c i t) -> p c t i", t=PACK, i=4),
+                both[0][:].rearrange("p (t c i) -> p c t i", t=PACK, i=4),
+                both[1][:].rearrange("p (t c i) -> p c t i", t=PACK, i=4),
+                ALU.add,
+            )
+            quantise(z2q, z2qs, lo, hi, grouped)
+            acc = turns.tile([P, hi - lo], F32, name="h_late%d" % c, tag="turn")
+            second_product(0, lo, hi, dealt_first, 0, acc[:])
+        dealt_rest = deal_second_weights(1, PACK, ("ring0", "ring1", "ring2"))
         for t in range(1, PACK):
-            h_out(t, 0, S)
+            second_product(t, 0, S, dealt_rest, t - 1, h_ps[t][:])
 
         oq = sb("oq", S, U32)
         oqs = sb("oqs", S, U8)
@@ -299,5 +300,5 @@ def tile_picked_joinsendlerpquad_none_po_kernel(
             quantise(oq, oqs, lo, hi, res16)
             nc.sync.dma_start(out=out_words[:, lo:hi], in_=oq[:, lo:hi].bitcast(I32))
         for q in range(4):
-            queue = nc.sync if q % 2 == 0 else nc.scalar
+            queue = nc.sync if q == 0 else nc.scalar
             queue.dma_start(out=out_2[0, 4 * q : 4 * q + 4, :].bitcast(I32), in_=oqs[32 * q : 32 * q + 4, :].bitcast(I32))

@@ -20,6 +20,7 @@ P = 128
 PACK = 4
 STRIPE = 16
 CHUNKS = ((0, 256), (256, 384), (384, 512))
+HALVES = ((0, 256), (256, 512))
 
 
 def entries(tile, lo, hi):
@@ -106,24 +107,26 @@ def tile_picked_joinsendlerpquad_none_po_kernel(
         nc.scalar.activation(out=gn_half[:], in_=gains[:, 0:PACK], func=ACT.Copy, scale=-0.5)
 
         w1d = sb("w1d", H, I32)
-        w1ds = sb("w1ds", H, U8)
+        w1ds = [sb("w1ds_first", P, U8), sb("w1ds_rest", H - P, U8)]
         deal_columns(nc, w1d, w1w, 4)
         xg = sb("xg", S, U32)
         xgs = sb("xgs", S, U8)
         nc.vector.tensor_copy(out=xgs[:], in_=xs[:].indirect(l0[:]))
-        deal_columns(nc, w1ds, w1s, 16)
+        deal_columns(nc, w1ds[0], w1s, 16, 0, 1)
         halves = ((0, S // 2), (S // 2, S))
         for lo, hi in halves:
             nc.vector.tensor_copy(out=xg[:, lo:hi], in_=xw[:].bitcast(U32).indirect(entries(l0, lo, hi)))
+        deal_columns(nc, w1ds[1], w1s, 16, 1, PACK)
 
         y_ps = [sums.tile([P, S], F32, name="y_ps%d" % t, tag="sum%d" % t) for t in range(PACK)]
         rl = [sb("rl%d" % t, S, F32) for t in range(PACK)]
         ds = [sb("ds%d" % t, 2 * S, F32) for t in range(PACK)]
         for t in range(PACK):
             cols = slice(P * t, P * (t + 1))
+            w1_scale = w1ds[0][:] if t == 0 else w1ds[1][:, P * (t - 1) : P * t]
             for lo, hi in halves if t == 0 else ((0, S),):
                 nc.tensor.matmul_mx(
-                    out=y_ps[t][:, lo:hi], lhsT=w1d[:, cols].bitcast(FP8X4), lhsT_scale=w1ds[:, cols],
+                    out=y_ps[t][:, lo:hi], lhsT=w1d[:, cols].bitcast(FP8X4), lhsT_scale=w1_scale,
                     rhs=xg[:, lo:hi].bitcast(FP8X4), rhs_scale=xgs[:, lo:hi], start=True, stop=True,
                 )
                 nc.scalar.activation(out=rl[t][:, lo:hi], in_=y_ps[t][:, lo:hi], func=ACT.Relu)
@@ -147,11 +150,11 @@ def tile_picked_joinsendlerpquad_none_po_kernel(
         y = [sb("y%d" % t, S, F32) for t in range(PACK)]
         yg = [sb("yg%d" % t, S, F32) for t in range(PACK)]
         yh = [sb("yh%d" % t, S, F32) for t in range(PACK)]
-        gate = [sb("gate%d" % c, PACK * (hi - lo), F32) for c, (lo, hi) in enumerate(CHUNKS)]
-        rest = [sb("rest%d" % c, PACK * (hi - lo), F32) for c, (lo, hi) in enumerate(CHUNKS)]
+        gate = [sb("gate%d" % c, PACK * (hi - lo), F32) for c, (lo, hi) in enumerate(HALVES)]
+        rest = [sb("rest%d" % c, PACK * (hi - lo), F32) for c, (lo, hi) in enumerate(HALVES)]
 
         def gate_of(c, t):
-            lo, hi = CHUNKS[c]
+            lo, hi = HALVES[c]
             w = hi - lo
             nc.scalar.activation(
                 out=gate[c][:, w * t : w * (t + 1)], in_=y[t][:].indirect(entries(l3, lo, hi)), func=ACT.Sigmoid,
@@ -176,12 +179,13 @@ def tile_picked_joinsendlerpquad_none_po_kernel(
             w = hi - lo
             far = sb("far%d" % c, PACK * w, F32, tag_b)
             near = sb("near%d" % c, PACK * w, F32, tag_a)
+            half, at = divmod(lo, S // 2)
             for t in range(PACK):
                 cols = slice(w * t, w * (t + 1))
-                nc.vector.tensor_tensor(far[:, cols], yg[t][:].indirect(entries(l4, lo, hi)), gate[c][:, cols], ALU.mult)
+                nc.vector.tensor_tensor(far[:, cols], yg[t][:].indirect(entries(l4, lo, hi)), gate[half][:, 256 * t + at : 256 * t + at + w], ALU.mult)
             for t in range(PACK):
                 cols = slice(w * t, w * (t + 1))
-                nc.vector.tensor_tensor(near[:, cols], yg[t][:].indirect(entries(l2, lo, hi)), rest[c][:, cols], ALU.mult)
+                nc.vector.tensor_tensor(near[:, cols], yg[t][:].indirect(entries(l2, lo, hi)), rest[half][:, 256 * t + at : 256 * t + at + w], ALU.mult)
             return far, near
 
         def add_turned(pairs, blocks, name):
@@ -232,9 +236,6 @@ def tile_picked_joinsendlerpquad_none_po_kernel(
         terms1 = terms(1, None, None)
         for a, (lo, hi) in enumerate(halves):
             quantise(zq, zqs, lo, hi, round_and_turn_back(z_banks[2 * a : 2 * a + 2], "z%d" % a, "ring%d" % a))
-        for t in range(PACK):
-            gate_of(2, t)
-        rest_of(2)
         terms2 = terms(2, "ring1", "ring0")
 
         h_ps = [sums.tile([P, S], F32, name="h_ps%d" % t, tag="sum%d" % t) for t in range(PACK)]

from contextlib import ExitStack

import concourse.mybir as mybir
from concourse.masks import make_identity

K, T, S, H, N = 512, 2048, 512, 512, 512
FLOPS = 2 * K * H * S + 2 * 2 * H * N * S

F32 = mybir.dt.float32
BF16 = mybir.dt.bfloat16
I32 = mybir.dt.int32
U32 = mybir.dt.uint32
U16 = mybir.dt.uint16
U8 = mybir.dt.uint8
FP8X4 = mybir.dt.float8_e4m3fn_x4
ALU = mybir.AluOpType
ACT = mybir.ActivationFunctionType

P = 128
PACK = 4
STRIPE = 16
CHUNKS = ((0, 256), (256, 384), (384, 512))
HALVES = ((0, 256), (256, 512))


def entries(tile, lo, hi):
    return tile[:, lo // STRIPE : hi // STRIPE]


def load_words(nc, tile, words):
    nc.sync.dma_start(out=tile[:], in_=words[0].rearrange("p n t -> p (n t)").bitcast(I32))


def load_scales(queues, tile, scales, first):
    for q, queue in enumerate(queues):
        queue.dma_start(
            out=tile[32 * q + first : 32 * q + first + 4, :].bitcast(I32),
            in_=scales[0, 4 * q : 4 * q + 4, :].bitcast(I32),
        )


def deal_columns(nc, dst, src, run, first=0, last=PACK):
    nc.vector.tensor_copy(
        out=dst[:].rearrange("p (t c i) -> p c t i", t=last - first, i=run),
        in_=src[:].rearrange("p (c i t) -> p c t i", t=PACK, i=run)[:, :, first:last, :],
    )


def tile_picked_joinsendlerpquad_none_po_kernel(
    tc, x_words, x_scales, w1_words, w1_scales, gn, gm, w2_words, w2_scales, w3_words, w3_scales,
    offs, n1, n2, n3, n4, n5, n6, out_0, out_1, out_2,
):
    nc = tc.nc
    with ExitStack() as ctx:
        keep = ctx.enter_context(tc.tile_pool(name="keep", bufs=1))
        sums = ctx.enter_context(tc.psum_pool(name="sums", bufs=1))
        turns = ctx.enter_context(tc.psum_pool(name="turns", bufs=4))

        def sb(name, width, dtype, tag=None):
            return keep.tile([P, width], dtype, name=name, tag=tag or name, align_bytes=64)

        xw = sb("xw", T, I32)
        xs = sb("xs", T, U8)
        w1w = sb("w1w", H, I32)
        w1s = sb("w1s", H, U8)
        w2w = sb("w2w", N, I32)
        w3w = sb("w3w", N, I32)
        w23s = sb("w23s", N, U8)
        gains = sb("gains", PACK, F32)
        gains_m = sb("gains_m", PACK, F32)
        lists = [keep.tile([P, S // STRIPE], U16, name="list%d" % a) for a in range(7)]
        l0, l1, l2, l3, l4, l5, l6 = lists

        nc.gpsimd.memset(xs[:].bitcast(I32), 0)
        nc.gpsimd.memset(w1s[:].bitcast(I32), 0)
        nc.gpsimd.dma_start(out=gains[:], in_=gn.rearrange("(p t) o -> p (t o)", t=PACK))
        nc.vector.memset(w23s[:].bitcast(I32), 0)
        warm = sb("warm", 2, F32)
        nc.vector.memset(warm[:, 0:1], 0.0)
        nc.scalar.activation(out=warm[:, 1:2], in_=warm[:, 0:1], func=ACT.Sigmoid)

        on_sync = [nc.sync] * 4
        load_scales(on_sync, xs, x_scales, 0)
        nc.sync.dma_start(l0[:], offs)
        load_words(nc, w1w, w1_words)
        load_words(nc, xw, x_words)
        load_scales(on_sync, w1s, w1_scales, 0)
        nc.sync.dma_start(l1[:], n1)
        nc.sync.dma_start(out=gains_m[:], in_=gm.rearrange("(p t) o -> p (t o)", t=PACK))
        nc.sync.dma_start(l3[:], n3)
        load_words(nc, w2w, w2_words)
        load_words(nc, w3w, w3_words)
        load_scales(on_sync, w23s, w2_scales, 0)
        load_scales(on_sync, w23s, w3_scales, 4)
        nc.sync.dma_start(l4[:], n4)
        nc.sync.dma_start(l2[:], n2)
        nc.sync.dma_start(l5[:], n5)
        nc.sync.dma_start(l6[:], n6)

        ident = sb("ident", P, F32)
        make_identity(nc, ident[:])

        gn_wide = [sb("gn_wide%d" % t, S, F32) for t in range(PACK)]
        for t in range(PACK):
            nc.scalar.copy(out=gn_wide[t][:], in_=gains[:, t : t + 1].to_broadcast([P, S]))
        gn_half = sb("gn_half", PACK, F32)
        nc.scalar.activation(out=gn_half[:], in_=gains[:, 0:PACK], func=ACT.Copy, scale=-0.5)

        w1d = sb("w1d", H, I32)
        w1ds = [sb("w1ds_first", P, U8), sb("w1ds_rest", H - P, U8)]
        deal_columns(nc, w1d, w1w, 4)
        xg = sb("xg", S, U32)
        xgs = sb("xgs", S, U8)
        nc.vector.tensor_copy(out=xgs[:], in_=xs[:].indirect(l0[:]))
        deal_columns(nc, w1ds[0], w1s, 16, 0, 1)
        halves = ((0, S // 2), (S // 2, S))
        for lo, hi in halves:
            nc.vector.tensor_copy(out=xg[:, lo:hi], in_=xw[:].bitcast(U32).indirect(entries(l0, lo, hi)))
        deal_columns(nc, w1ds[1], w1s, 16, 1, PACK)

        y_ps = [sums.tile([P, S], F32, name="y_ps%d" % t, tag="sum%d" % t) for t in range(PACK)]
        rl = [sb("rl%d" % t, S, F32) for t in range(PACK)]
        ds = [sb("ds%d" % t, 2 * S, F32) for t in range(PACK)]
        for t in range(PACK):
            cols = slice(P * t, P * (t + 1))
            w1_scale = w1ds[0][:] if t == 0 else w1ds[1][:, P * (t - 1) : P * t]
            for lo, hi in halves if t == 0 else ((0, S),):
                nc.tensor.matmul_mx(
                    out=y_ps[t][:, lo:hi], lhsT=w1d[:, cols].bitcast(FP8X4), lhsT_scale=w1_scale,
                    rhs=xg[:, lo:hi].bitcast(FP8X4), rhs_scale=xgs[:, lo:hi], start=True, stop=True,
                )
                nc.scalar.activation(out=rl[t][:, lo:hi], in_=y_ps[t][:, lo:hi], func=ACT.Relu)
                nc.vector.tensor_tensor(
                    ds[t][:].indirect(entries(l1, lo, hi)), rl[t][:, lo:hi],
                    gn_wide[t][:, lo:hi], ALU.mult,
                )

        def deal_second_weights(first, last, tags):
            w = P * (last - first)
            w2d = sb("w2d%d" % first, w, I32, tags[0])
            w3d = sb("w3d%d" % first, w, I32, tags[1])
            w23ds = sb("w23ds%d" % first, w, U8, tags[2])
            deal_columns(nc, w2d, w2w, 4, first, last)
            deal_columns(nc, w3d, w3w, 4, first, last)
            deal_columns(nc, w23ds, w23s, 16, first, last)
            return w2d, w3d, w23ds

        dealt_first = deal_second_weights(0, 1, (None, None, None))

        y = [sb("y%d" % t, S, F32) for t in range(PACK)]
        yg = [sb("yg%d" % t, S, F32) for t in range(PACK)]
        yh = [sb("yh%d" % t, S, F32) for t in range(PACK)]
        gate = [sb("gate%d" % c, PACK * (hi - lo), F32) for c, (lo, hi) in enumerate(HALVES)]
        rest = [sb("rest%d" % c, PACK * (hi - lo), F32) for c, (lo, hi) in enumerate(HALVES)]

        def gate_of(c, t):
            lo, hi = HALVES[c]
            w = hi - lo
            nc.scalar.activation(
                out=gate[c][:, w * t : w * (t + 1)], in_=y[t][:].indirect(entries(l3, lo, hi)), func=ACT.Sigmoid,
            )

        def rest_of(c):
            nc.scalar.activation(out=rest[c][:], in_=gate[c][:], func=ACT.Copy, scale=-1.0, bias=1.0)

        for t in range(PACK):
            nc.scalar.copy(out=y[t][:], in_=y_ps[t][:])
            nc.scalar.activation(out=yg[t][:], in_=y_ps[t][:], func=ACT.Copy, scale=gains_m[:, t : t + 1])
            gate_of(0, t)
        rest_of(0)
        for t in range(PACK):
            nc.scalar.activation(out=yh[t][:], in_=y_ps[t][:], func=ACT.Copy, scale=gn_half[:, t : t + 1])
        for t in range(PACK):
            gate_of(1, t)
        rest_of(1)

        def terms(c, tag_a, tag_b):
            lo, hi = CHUNKS[c]
            w = hi - lo
            far = sb("far%d" % c, PACK * w, F32, tag_b)
            near = sb("near%d" % c, PACK * w, F32, tag_a)
            half, at = divmod(lo, S // 2)
            for t in range(PACK):
                cols = slice(w * t, w * (t + 1))
                nc.vector.tensor_tensor(far[:, cols], yg[t][:].indirect(entries(l4, lo, hi)), gate[half][:, 256 * t + at : 256 * t + at + w], ALU.mult)
            for t in range(PACK):
                cols = slice(w * t, w * (t + 1))
                nc.vector.tensor_tensor(near[:, cols], yg[t][:].indirect(entries(l2, lo, hi)), rest[half][:, 256 * t + at : 256 * t + at + w], ALU.mult)
            return far, near

        def add_turned(pairs, blocks, name):
            banks = [turns.tile([P, PACK * P], F32, name="%s_sum%d" % (name, b), tag="turn") for b in blocks]
            for t in range(PACK):
                for bank, b in zip(banks, blocks):
                    for a in range(2):
                        nc.tensor.matmul(
                            bank[:, P * t : P * (t + 1)], pairs[t][a][:, P * b : P * (b + 1)], ident[:],
                            start=(a == 0), stop=(a == 1), is_transpose=True,
                        )
            return banks

        def round_and_turn_back(banks, name, tag):
            turned = []
            for b, bank in enumerate(banks):
                pairs16 = sb("%s_pairs%d" % (name, b), PACK * P, BF16)
                nc.scalar.copy(
                    out=pairs16[:].rearrange("j (u p e) -> j u p e", u=2, e=2),
                    in_=bank[:].rearrange("j (u e p) -> j u p e", u=2, e=2),
                )
                turned.append(pairs16)
            w = P * len(banks)
            back = turns.tile([P, 2 * w], F32, name="%s_back" % name, tag="turn")
            for b, pairs16 in enumerate(turned):
                for u in range(2):
                    nc.tensor.transpose(
                        back[:, w * u + P * b : w * u + P * (b + 1)],
                        pairs16[:].bitcast(F32)[:, P * u : P * (u + 1)], ident[:],
                    )
            grouped = sb("%s_grouped" % name, PACK * w, BF16, tag)
            nc.scalar.copy(
                out=grouped[:].bitcast(F32).rearrange("p (j u) -> p j u", u=2),
                in_=back[:].rearrange("p (u j) -> p j u", u=2),
            )
            return grouped

        def quantise(words, scales, lo, hi, grouped):
            nc.vector.quantize_mx(out=words[:, lo:hi].bitcast(FP8X4), scales=scales[:, lo:hi], in_=grouped[:])

        zq = sb("zq", S, U32)
        zqs = sb("zqs", S, U8)
        z2q = sb("z2q", S, U32)
        z2qs = sb("z2qs", S, U8)

        z_banks = add_turned([[yh[t][:], ds[t][:, 0:S]] for t in range(PACK)], range(4), "z")
        terms0 = terms(0, None, None)
        terms1 = terms(1, None, None)
        for a, (lo, hi) in enumerate(halves):
            quantise(zq, zqs, lo, hi, round_and_turn_back(z_banks[2 * a : 2 * a + 2], "z%d" % a, "ring%d" % a))
        terms2 = terms(2, "ring1", "ring0")

        h_ps = [sums.tile([P, S], F32, name="h_ps%d" % t, tag="sum%d" % t) for t in range(PACK)]
        h = [sb("h%d" % t, S, F32) for t in range(PACK)]
        h_own = [sb("h_own%d" % t, S, F32) for t in range(PACK)]

        def second_product(t, lo, hi, dealt, at, acc):
            w2d, w3d, w23ds = dealt
            cols = slice(P * at, P * (at + 1))
            nc.tensor.matmul_mx(
                out=acc, lhsT=w2d[:, cols].bitcast(FP8X4), lhsT_scale=w23ds[:, cols],
                rhs=zq[:, lo:hi].bitcast(FP8X4), rhs_scale=zqs[:, lo:hi], start=True, stop=False,
            )
            nc.tensor.matmul_mx(
                out=acc, lhsT=w3d[:, cols].bitcast(FP8X4), lhsT_scale=w23ds[4:P, cols],
                rhs=z2q[:, lo:hi].bitcast(FP8X4), rhs_scale=z2qs[:, lo:hi], start=False, stop=True,
            )
            nc.scalar.copy(out=h[t][:, lo:hi], in_=acc)
            nc.scalar.copy(out=h_own[t][:, lo:hi], in_=acc)

        lo, hi = CHUNKS[0]
        pairs = [[term[:, (hi - lo) * t : (hi - lo) * (t + 1)] for term in terms0] for t in range(PACK)]
        banks = add_turned(pairs, range((hi - lo) // P), "z2")
        quantise(z2q, z2qs, lo, hi, round_and_turn_back(banks, "z2", "ring2"))
        second_product(0, lo, hi, dealt_first, 0, h_ps[0][:, lo:hi])
        for c, both in ((1, terms1), (2, terms2)):
            lo, hi = CHUNKS[c]
            grouped = sb("z2_grouped%d" % c, PACK * (hi - lo), BF16, "ring2" if c == 2 else None)
            nc.vector.tensor_tensor(
                grouped[:].rearrange("p (c i t) -> p c t i", t=PACK, i=4),
                both[0][:].rearrange("p (t c i) -> p c t i", t=PACK, i=4),
                both[1][:].rearrange("p (t c i) -> p c t i", t=PACK, i=4),
                ALU.add,
            )
            quantise(z2q, z2qs, lo, hi, grouped)
            acc = turns.tile([P, hi - lo], F32, name="h_late%d" % c, tag="turn")
            second_product(0, lo, hi, dealt_first, 0, acc[:])
        dealt_rest = deal_second_weights(1, PACK, ("ring0", "ring1", "ring2"))
        for t in range(1, PACK):
            second_product(t, 0, S, dealt_rest, t - 1, h_ps[t][:])

        oq = sb("oq", S, U32)
        oqs = sb("oqs", S, U8)
        out_rows = out_0.rearrange("(p t) j -> p t j", t=PACK)
        out_words = out_1[0].rearrange("p n t -> p (n t)").bitcast(I32)
        for c, (lo, hi) in enumerate(CHUNKS):
            w = hi - lo
            d5 = sb("d5_%d" % c, PACK * w, F32)
            d6 = sb("d6_%d" % c, PACK * w, F32)
            res = sb("res%d" % c, PACK * w, F32)
            for t in range(PACK):
                cols = slice(w * t, w * (t + 1))
                nc.vector.tensor_tensor(d5[:, cols], h[t][:].indirect(entries(l5, lo, hi)), h_own[t][:, lo:hi], ALU.subtract)
                nc.vector.tensor_tensor(d6[:, cols], h[t][:].indirect(entries(l6, lo, hi)), h_own[t][:, lo:hi], ALU.subtract)
            nc.vector.scalar_tensor_tensor(out=res[:], in0=d5[:], scalar=0.75, in1=d6[:], op0=ALU.mult, op1=ALU.mult)
            nc.sync.dma_start(out=out_rows[:, :, lo:hi], in_=res[:].rearrange("p (t j) -> p t j", t=PACK))
            res16 = sb("res16_%d" % c, PACK * w, BF16)
            copy = nc.vector.tensor_copy if c == len(CHUNKS) - 1 else nc.scalar.copy
            copy(
                out=res16[:].rearrange("p (c i t) -> p c t i", t=PACK, i=4),
                in_=res[:].rearrange("p (t c i) -> p c t i", t=PACK, i=4),
            )
            quantise(oq, oqs, lo, hi, res16)
            nc.sync.dma_start(out=out_words[:, lo:hi], in_=oq[:, lo:hi].bitcast(I32))
        for q in range(4):
            queue = nc.sync if q == 0 else nc.scalar
            queue.dma_start(out=out_2[0, 4 * q : 4 * q + 4, :].bitcast(I32), in_=oqs[32 * q : 32 * q + 4, :].bitcast(I32))
